import numpy as np
import ml_dtypes


def mxq(x, axis, fmt="e4m3"):
    dtype, down = {"e4m3": (ml_dtypes.float8_e4m3fn, 7), "e5m2": (ml_dtypes.float8_e5m2, 14)}[fmt]
    v = np.moveaxis(np.asarray(x, np.float32).astype(ml_dtypes.bfloat16).astype(np.float64), axis, -1)
    blocks = v.reshape(v.shape[:-1] + (-1, 32))
    amax = np.abs(blocks).max(-1, keepdims=True)
    byte = np.maximum(np.where(amax > 0, np.frexp(amax)[1] - 1 + 127, 0) - down, 1)
    scale = np.exp2(byte - 127.0)
    codes = (blocks / scale).astype(np.float32).astype(dtype).astype(np.float64)
    return np.moveaxis((codes * scale).reshape(v.shape), -1, axis)


WIDE = False


def mx_kscale(k):
    if not WIDE:
        return np.ones(k)
    levels = np.array([10, -10, 5, -5, 0])
    if k % 512:
        return np.exp2(np.random.permutation(np.resize(levels, k // 32))).repeat(32)
    a = np.empty((k // 512, 16))
    for p in range(k // 512):
        a[p, :8] = np.random.permutation(np.resize(levels, 8))
        for g in range(8):
            far = levels[np.abs(levels - a[p, g]) >= 10]
            a[p, g + 8] = far[np.random.randint(len(far))]
    return np.exp2(a.ravel()).repeat(32)


def f64(x):
    return np.asarray(x).astype(np.float64)


def striped(idx):
    return np.tile(idx.reshape(-1, 16).T, (8, 1)).astype(np.uint16)


def unstriped(offs):
    return offs[:16].T.reshape(-1).astype(np.int64)


def pack_weight(w):
    k, n = w.shape
    w = f64(np.asarray(w, np.float32).astype(ml_dtypes.bfloat16)).reshape(k // 32, 32, n)
    amax = np.abs(w).max(1)
    byte = np.clip(np.where(amax > 0, np.frexp(amax)[1] - 1 + 127 - 7, 1), 1, 254)
    scaled = (w * np.exp2(127.0 - byte)[:, None, :]).reshape(k, n).astype(np.float32)
    words = np.ascontiguousarray(scaled.reshape(k // 512, 128, 4, n).transpose(0, 1, 3, 2)).astype(ml_dtypes.float8_e4m3fn).view(np.uint8)
    return words, np.ascontiguousarray(byte.astype(np.uint8).reshape(k // 512, 16, n))


def unpack_weight(words, scales):
    g, p, n, _ = words.shape
    vals = np.ascontiguousarray(words).view(ml_dtypes.float8_e4m3fn).astype(np.float64) * np.repeat(np.exp2(scales.astype(np.float64) - 127.0), 8, axis=1)[..., None]
    return vals.transpose(0, 1, 3, 2).reshape(g * 512, n)


def gelu(v):
    return 0.5 * v * (1.0 + np.tanh(np.sqrt(2.0 / np.pi) * (v + 0.044715 * v**3)))


K, T, S, N, H, W = 512, 1024, 512, 256, 512, 1024


def setup_inputs():
    n = np.random.standard_normal
    s = mx_kscale(K)[:, None]
    u = mx_kscale(H)
    packed_xT = pack_weight(n((K, T)) * s)
    packed_eT = pack_weight(n((K, W)) * s)
    return {
        "x_words": packed_xT[0],
        "x_scales": packed_xT[1],
        "w1": (n((K, H)) / np.sqrt(K) / s).astype(np.float32),
        "e_words": packed_eT[0],
        "e_scales": packed_eT[1],
        "w2": (n((K, H)) / np.sqrt(K) / s).astype(np.float32),
        "mag": (np.random.uniform(0.5, 1.6, (H, 1))).astype(np.float32),
        "unit": (np.random.uniform(0.6, 1.4, (H, 1)) * u[:, None]).astype(np.float32),
        "w3": (n((H, N)) / np.sqrt(H) / u[:, None]).astype(np.float32),
        "offs": striped(np.random.permutation(T)[:S]),
        "adp": striped(np.random.permutation(W)[:S]),
    }


def reference(x_words, x_scales, w1, e_words, e_scales, w2, mag, unit, w3, offs, adp):
    xq = unpack_weight(x_words, x_scales)[:, unstriped(offs)]
    y = mxq(f64(w1), 0, "e4m3").T @ xq
    e_adp = unpack_weight(e_words, e_scales)[:, unstriped(adp)]
    ye = mxq(f64(w2), 0, "e4m3").T @ e_adp
    drc = y + 0.7 * ye
    wsq = (drc) ** 2
    msq = wsq.mean(axis=1, keepdims=True)
    nrm = np.sqrt(msq + 0.1)
    out1 = f64(mag) * (drc / nrm)
    hid = f64(unit) * gelu(out1)
    return mxq(f64(w3), 0, "e4m3").T @ mxq(hid, 0, "e4m3")

@@ -1,0 +1,185 @@
+import math
+from contextlib import ExitStack
+
+import concourse.mybir as mybir
+
+K, T, S, N, H = 512, 1024, 512, 256, 512
+FLOPS = 2 * K * H * S * 2 + 2 * H * N * S
+
+F32 = mybir.dt.float32
+BF16 = mybir.dt.bfloat16
+I32 = mybir.dt.int32
+U32 = mybir.dt.uint32
+U16 = mybir.dt.uint16
+U8 = mybir.dt.uint8
+FP8X4 = mybir.dt.float8_e4m3fn_x4
+ALU = mybir.AluOpType
+ACT = mybir.ActivationFunctionType
+
+P = 128
+PACK = 4
+HALF = 256
+
+
+def tile_picked_ydorax_gelu_p_kernel(
+    tc, x_words, x_scales, w1, e_words, e_scales, w2, mag, unit, w3, offs, adp, out
+):
+    nc = tc.nc
+    with ExitStack() as ctx:
+        keep = ctx.enter_context(tc.tile_pool(name="keep", bufs=1))
+        psum = ctx.enter_context(tc.psum_pool(name="psum", bufs=1))
+
+        def sb(name, shape, dtype):
+            return keep.tile(shape, dtype, name=name, align_bytes=64)
+
+        x_list = sb("x_list", [P, S // 16], U16)
+        e_list = sb("e_list", [P, S // 16], U16)
+        x_word_table = sb("x_word_table", [P, T], U32)
+        e_word_table = sb("e_word_table", [P, T], U32)
+        x_scale_table = sb("x_scale_table", [P, T], U8)
+        e_scale_table = sb("e_scale_table", [P, T], U8)
+        w1_raw = [sb(f"w1_raw{h}", [P, PACK, HALF], F32) for h in range(2)]
+        w2_raw = [sb(f"w2_raw{h}", [P, PACK, HALF], F32) for h in range(2)]
+        w3_raw = sb("w3_raw", [P, PACK, N], F32)
+        mag_sb = sb("mag_sb", [P, PACK], F32)
+        unit_sb = sb("unit_sb", [P, PACK], F32)
+        minus_half = sb("minus_half", [P, 1], F32)
+
+        def load_scale_rows(queue, table, scales):
+            rows = scales[0].bitcast(I32)
+            for q in range(4):
+                queue.dma_start(out=table[32 * q : 32 * q + 4, :].bitcast(I32), in_=rows[4 * q : 4 * q + 4, :])
+
+        def load_words(table, words):
+            nc.sync.dma_start(out=table[:].bitcast(I32), in_=words[0].rearrange("p n r -> p (n r)").bitcast(I32))
+
+        def load_half(raw, w, h):
+            nc.sync.dma_start(out=raw[h][:], in_=w.rearrange("(p j) c -> p j c", j=PACK)[:, :, h * HALF : (h + 1) * HALF])
+
+        nc.gpsimd.memset(x_scale_table[:].bitcast(I32), 0)
+        nc.vector.memset(e_scale_table[:].bitcast(I32), 0)
+        nc.sync.dma_start(x_list[:], offs)
+        nc.sync.dma_start(e_list[:], adp)
+        load_half(w1_raw, w1, 0)
+        load_scale_rows(nc.sync, x_scale_table, x_scales)
+        load_half(w1_raw, w1, 1)
+        load_scale_rows(nc.sync, e_scale_table, e_scales)
+        load_words(x_word_table, x_words)
+        load_half(w2_raw, w2, 0)
+        load_words(e_word_table, e_words)
+        load_half(w2_raw, w2, 1)
+        nc.sync.dma_start(out=w3_raw[:], in_=w3.rearrange("(p j) c -> p j c", j=PACK))
+        nc.sync.dma_start(out=mag_sb[:], in_=mag.rearrange("(p t) o -> p (t o)", t=PACK))
+        nc.sync.dma_start(out=unit_sb[:], in_=unit.rearrange("(p t) o -> p (t o)", t=PACK))
+        nc.gpsimd.memset(minus_half[:], -0.5)
+        drc = sb("drc", [P, PACK, S + 16], F32)
+        ones = sb("ones", [P, PACK], F32)
+        nc.gpsimd.memset(ones[:], 1.0)
+        nc.gpsimd.tensor_scalar(
+            out=drc[:, :, S], in0=ones[:], scalar1=math.sqrt(0.1 * S), scalar2=0.0, op0=ALU.mult, op1=ALU.add
+        )
+
+        def deal_half(copy, grouped, raw, h):
+            m_half = slice(h * HALF // PACK, (h + 1) * HALF // PACK)
+            copy(
+                out=grouped[:].rearrange("p t m j -> p m j t")[:, m_half],
+                in_=raw[h][:].rearrange("p j (m t) -> p m j t", t=PACK),
+            )
+
+        def quantize(name, grouped_flat, width):
+            codes = sb(name + "_codes", [P, width], U32)
+            scales = sb(name + "_scales", [P, width], U8)
+            nc.vector.quantize_mx(out=codes[:].bitcast(FP8X4), scales=scales[:], in_=grouped_flat)
+            return codes, scales
+
+        def gather(name, table, offsets, dtype):
+            picked = sb(name, [P, S], dtype)
+            nc.vector.tensor_copy(out=picked[:], in_=table[:].indirect(offsets[:]))
+            return picked
+
+        def product(acc, w_codes, w_scales, cols, codes, scales):
+            nc.tensor.matmul_mx(
+                out=acc,
+                lhsT=w_codes[:, cols].bitcast(FP8X4),
+                lhsT_scale=w_scales[:, cols],
+                rhs=codes.bitcast(FP8X4),
+                rhs_scale=scales,
+                start=True,
+                stop=True,
+            )
+
+        w1_grouped = sb("w1_grouped", [P, PACK, P, PACK], BF16)
+        w2_grouped = sb("w2_grouped", [P, PACK, P, PACK], BF16)
+        w3_grouped = sb("w3_grouped", [P, N, PACK], BF16)
+
+        x_scale_picked = gather("x_scale_picked", x_scale_table, x_list, U8)
+        deal_half(nc.scalar.copy, w1_grouped, w1_raw, 0)
+        deal_half(nc.scalar.copy, w1_grouped, w1_raw, 1)
+        e_scale_picked = gather("e_scale_picked", e_scale_table, e_list, U8)
+        x_word_picked = gather("x_word_picked", x_word_table, x_list, U32)
+        w1_q = [quantize(f"w1_{t}", w1_grouped[:, t].rearrange("p m j -> p (m j)"), P) for t in range(PACK)]
+        deal_half(nc.scalar.copy, w2_grouped, w2_raw, 0)
+
+        y_sb = []
+        for t in range(PACK):
+            y_bank = psum.tile([P, S], F32, name=f"y_bank{t}", tag=f"y_bank{t}")
+            product(y_bank[:], *w1_q[t], slice(0, P), x_word_picked[:], x_scale_picked[:])
+            y_t = sb(f"y_sb{t}", [P, S], F32)
+            nc.scalar.copy(out=y_t[:], in_=y_bank[:])
+            y_sb.append(y_t)
+
+        e_word_picked = gather("e_word_picked", e_word_table, e_list, U32)
+        deal_half(nc.vector.tensor_copy, w2_grouped, w2_raw, 1)
+        w2_q = [quantize(f"w2_{t}", w2_grouped[:, t].rearrange("p m j -> p (m j)"), P) for t in range(PACK)]
+
+        inv_nrm = []
+        for t in range(PACK):
+            ye_bank = psum.tile([P, S], F32, name=f"ye_bank{t}", tag=f"ye_bank{t}")
+            product(ye_bank[:], *w2_q[t], slice(0, P), e_word_picked[:], e_scale_picked[:])
+            nc.vector.scalar_tensor_tensor(out=drc[:, t, :S], in0=ye_bank[:], scalar=0.7, in1=y_sb[t][:], op0=ALU.mult, op1=ALU.add)
+            squares = sb(f"squares{t}", [P, S + 1], F32)
+            nrm_sq = sb(f"nrm_sq{t}", [P, 1], F32)
+            row = drc[:, t, : S + 1]
+            if t < PACK - 1:
+                nc.scalar.activation(out=squares[:], in_=row, func=ACT.Square, scale=1.0 / math.sqrt(S), accum_out=nrm_sq[:])
+            else:
+                nc.vector.scalar_tensor_tensor(
+                    out=squares[:], in0=row, scalar=1.0 / S, in1=row, op0=ALU.mult, op1=ALU.mult, accum_out=nrm_sq[:]
+                )
+            inv_t = sb(f"inv_nrm{t}", [P, 1], F32)
+            nc.gpsimd.tensor_tensor(out=inv_t[:], in0=nrm_sq[:], in1=minus_half[:], op=ALU.pow)
+            inv_nrm.append(inv_t)
+
+        nc.vector.tensor_copy(
+            out=w3_grouped[:].rearrange("p (c i) j -> p c j i", i=4),
+            in_=w3_raw[:].rearrange("p j (c i) -> p c j i", i=4),
+        )
+        w3_codes, w3_scales = quantize("w3", w3_grouped[:].rearrange("p n j -> p (n j)"), N)
+
+        hid = sb("hid", [P, PACK, S], BF16)
+        for t in range(PACK):
+            gain_t = sb(f"gain{t}", [P, 1], F32)
+            nc.vector.tensor_tensor(out=gain_t[:], in0=inv_nrm[t][:], in1=mag_sb[:, t : t + 1], op=ALU.mult)
+            act_t = sb(f"act{t}", [P, S], F32)
+            nc.scalar.activation(out=act_t[:], in_=drc[:, t, :S], func=ACT.Gelu_apprx_tanh, scale=gain_t[:])
+            nc.vector.tensor_scalar(out=hid[:, t, :], in0=act_t[:], scalar1=unit_sb[:, t : t + 1], scalar2=None, op0=ALU.mult)
+
+        hid_q = []
+        for h in range(2):
+            grouped = sb(f"hid_grouped{h}", [P, HALF, PACK], BF16)
+            copy = nc.vector.tensor_copy if h == 0 else nc.scalar.copy
+            copy(
+                out=grouped[:].rearrange("p (c i) t -> p c t i", i=4),
+                in_=hid[:, :, h * HALF : (h + 1) * HALF].rearrange("p t (c i) -> p c t i", i=4),
+            )
+            hid_q.append(quantize(f"hid{h}", grouped[:].rearrange("p n t -> p (n t)"), HALF))
+
+        for h in range(2):
+            codes, scales = hid_q[h]
+            for m in range(N // P):
+                bank = psum.tile([P, HALF], F32, name=f"out_bank{h}{m}", tag=f"y_bank{2 * h + m}")
+                product(bank[:], w3_codes, w3_scales, slice(m * P, (m + 1) * P), codes[:], scales[:])
+                result = sb(f"result{h}{m}", [P, HALF], F32)
+                copy = nc.scalar.copy if m == 0 else nc.vector.tensor_copy
+                copy(out=result[:], in_=bank[:])
+                nc.sync.dma_start(out=out[m * P : (m + 1) * P, h * HALF : (h + 1) * HALF], in_=result[:])

@@ -29,8 +29,8 @@ def tile_picked_ydorax_gelu_p_kernel(
         keep = ctx.enter_context(tc.tile_pool(name="keep", bufs=1))
         psum = ctx.enter_context(tc.psum_pool(name="psum", bufs=1))
 
-        def sb(name, shape, dtype):
-            return keep.tile(shape, dtype, name=name, align_bytes=64)
+        def sb(name, shape, dtype, tag=None):
+            return keep.tile(shape, dtype, name=name, tag=tag or name, align_bytes=64)
 
         x_list = sb("x_list", [P, S // 16], U16)
         e_list = sb("e_list", [P, S // 16], U16)
@@ -45,9 +45,9 @@ def tile_picked_ydorax_gelu_p_kernel(
         unit_sb = sb("unit_sb", [P, PACK], F32)
         minus_half = sb("minus_half", [P, 1], F32)
 
-        def load_scale_rows(queue, table, scales):
+        def load_scale_rows(queue, table, scales, quadrants):
             rows = scales[0].bitcast(I32)
-            for q in range(4):
+            for q in quadrants:
                 queue.dma_start(out=table[32 * q : 32 * q + 4, :].bitcast(I32), in_=rows[4 * q : 4 * q + 4, :])
 
         def load_words(table, words):
@@ -56,21 +56,21 @@ def tile_picked_ydorax_gelu_p_kernel(
         def load_half(raw, w, h):
             nc.sync.dma_start(out=raw[h][:], in_=w.rearrange("(p j) c -> p j c", j=PACK)[:, :, h * HALF : (h + 1) * HALF])
 
-        nc.gpsimd.memset(x_scale_table[:].bitcast(I32), 0)
+        nc.vector.memset(x_scale_table[:].bitcast(I32), 0)
         nc.vector.memset(e_scale_table[:].bitcast(I32), 0)
         nc.sync.dma_start(x_list[:], offs)
         nc.sync.dma_start(e_list[:], adp)
-        load_half(w1_raw, w1, 0)
-        load_scale_rows(nc.sync, x_scale_table, x_scales)
-        load_half(w1_raw, w1, 1)
-        load_scale_rows(nc.sync, e_scale_table, e_scales)
         load_words(x_word_table, x_words)
+        load_scale_rows(nc.sync, x_scale_table, x_scales, range(4))
+        load_half(w1_raw, w1, 0)
+        load_half(w1_raw, w1, 1)
+        load_scale_rows(nc.sync, e_scale_table, e_scales, range(4))
         load_half(w2_raw, w2, 0)
         load_words(e_word_table, e_words)
         load_half(w2_raw, w2, 1)
         nc.sync.dma_start(out=w3_raw[:], in_=w3.rearrange("(p j) c -> p j c", j=PACK))
-        nc.sync.dma_start(out=mag_sb[:], in_=mag.rearrange("(p t) o -> p (t o)", t=PACK))
-        nc.sync.dma_start(out=unit_sb[:], in_=unit.rearrange("(p t) o -> p (t o)", t=PACK))
+        nc.gpsimd.dma_start(out=mag_sb[:], in_=mag.rearrange("(p t) o -> p (t o)", t=PACK))
+        nc.gpsimd.dma_start(out=unit_sb[:], in_=unit.rearrange("(p t) o -> p (t o)", t=PACK))
         nc.gpsimd.memset(minus_half[:], -0.5)
         drc = sb("drc", [P, PACK, S + 16], F32)
         ones = sb("ones", [P, PACK], F32)
@@ -110,39 +110,50 @@ def tile_picked_ydorax_gelu_p_kernel(
 
         w1_grouped = sb("w1_grouped", [P, PACK, P, PACK], BF16)
         w2_grouped = sb("w2_grouped", [P, PACK, P, PACK], BF16)
-        w3_grouped = sb("w3_grouped", [P, N, PACK], BF16)
 
+        x_word_picked = gather("x_word_picked", x_word_table, x_list, U32)
         x_scale_picked = gather("x_scale_picked", x_scale_table, x_list, U8)
         deal_half(nc.scalar.copy, w1_grouped, w1_raw, 0)
         deal_half(nc.scalar.copy, w1_grouped, w1_raw, 1)
         e_scale_picked = gather("e_scale_picked", e_scale_table, e_list, U8)
-        x_word_picked = gather("x_word_picked", x_word_table, x_list, U32)
         w1_q = [quantize(f"w1_{t}", w1_grouped[:, t].rearrange("p m j -> p (m j)"), P) for t in range(PACK)]
         deal_half(nc.scalar.copy, w2_grouped, w2_raw, 0)
 
-        y_sb = []
+        y_sb = sb("y_sb", [P, PACK, S], F32, tag="w2_raw0")
         for t in range(PACK):
             y_bank = psum.tile([P, S], F32, name=f"y_bank{t}", tag=f"y_bank{t}")
             product(y_bank[:], *w1_q[t], slice(0, P), x_word_picked[:], x_scale_picked[:])
-            y_t = sb(f"y_sb{t}", [P, S], F32)
-            nc.scalar.copy(out=y_t[:], in_=y_bank[:])
-            y_sb.append(y_t)
+            nc.scalar.copy(out=y_sb[:, t, :], in_=y_bank[:])
 
         e_word_picked = gather("e_word_picked", e_word_table, e_list, U32)
         deal_half(nc.vector.tensor_copy, w2_grouped, w2_raw, 1)
         w2_q = [quantize(f"w2_{t}", w2_grouped[:, t].rearrange("p m j -> p (m j)"), P) for t in range(PACK)]
 
-        inv_nrm = []
+        w3_grouped = sb("w3_grouped", [P, N, PACK], BF16)
+        nc.scalar.copy(
+            out=w3_grouped[:].rearrange("p (c i) j -> p c j i", i=4),
+            in_=w3_raw[:].rearrange("p j (c i) -> p c j i", i=4),
+        )
+
+        last = PACK - 1
+        inv_nrm, gain = [], {}
+
+        def make_gain(t, tile):
+            gain[t] = tile
+            nc.vector.tensor_tensor(out=tile, in0=inv_nrm[t][:], in1=mag_sb[:, t : t + 1], op=ALU.mult)
+
         for t in range(PACK):
             ye_bank = psum.tile([P, S], F32, name=f"ye_bank{t}", tag=f"ye_bank{t}")
             product(ye_bank[:], *w2_q[t], slice(0, P), e_word_picked[:], e_scale_picked[:])
-            nc.vector.scalar_tensor_tensor(out=drc[:, t, :S], in0=ye_bank[:], scalar=0.7, in1=y_sb[t][:], op0=ALU.mult, op1=ALU.add)
+            nc.vector.scalar_tensor_tensor(out=drc[:, t, :S], in0=ye_bank[:], scalar=0.7, in1=y_sb[:, t, :], op0=ALU.mult, op1=ALU.add)
             squares = sb(f"squares{t}", [P, S + 1], F32)
             nrm_sq = sb(f"nrm_sq{t}", [P, 1], F32)
             row = drc[:, t, : S + 1]
-            if t < PACK - 1:
+            if t < last:
                 nc.scalar.activation(out=squares[:], in_=row, func=ACT.Square, scale=1.0 / math.sqrt(S), accum_out=nrm_sq[:])
             else:
+                first_gain = sb("first_gain", [P, 1], F32, tag="w2_raw0")
+                make_gain(0, first_gain[:])
                 nc.vector.scalar_tensor_tensor(
                     out=squares[:], in0=row, scalar=1.0 / S, in1=row, op0=ALU.mult, op1=ALU.mult, accum_out=nrm_sq[:]
                 )
@@ -150,36 +161,55 @@ def tile_picked_ydorax_gelu_p_kernel(
             nc.gpsimd.tensor_tensor(out=inv_t[:], in0=nrm_sq[:], in1=minus_half[:], op=ALU.pow)
             inv_nrm.append(inv_t)
 
-        nc.vector.tensor_copy(
-            out=w3_grouped[:].rearrange("p (c i) j -> p c j i", i=4),
-            in_=w3_raw[:].rearrange("p j (c i) -> p c j i", i=4),
-        )
-        w3_codes, w3_scales = quantize("w3", w3_grouped[:].rearrange("p n j -> p (n j)"), N)
-
-        hid = sb("hid", [P, PACK, S], BF16)
+        scaled_last = sb("scaled_last", [P, S], F32)
+        nc.vector.tensor_scalar(out=scaled_last[:], in0=drc[:, last, :S], scalar1=mag_sb[:, last:], scalar2=None, op0=ALU.mult)
+        gain[last] = inv_nrm[last][:]
+        later_gains = sb("later_gains", [P, last - 1, 8], F32, tag=f"squares{last}")
+        hid = [sb(f"hid{h}", [P, PACK, HALF], BF16) for h in range(2)]
         for t in range(PACK):
-            gain_t = sb(f"gain{t}", [P, 1], F32)
-            nc.vector.tensor_tensor(out=gain_t[:], in0=inv_nrm[t][:], in1=mag_sb[:, t : t + 1], op=ALU.mult)
-            act_t = sb(f"act{t}", [P, S], F32)
-            nc.scalar.activation(out=act_t[:], in_=drc[:, t, :S], func=ACT.Gelu_apprx_tanh, scale=gain_t[:])
-            nc.vector.tensor_scalar(out=hid[:, t, :], in0=act_t[:], scalar1=unit_sb[:, t : t + 1], scalar2=None, op0=ALU.mult)
+            if 0 < t < last:
+                make_gain(t, later_gains[:, t - 1, 0:1])
+            if t == 1:
+                w3_codes, w3_scales = quantize("w3", w3_grouped[:].rearrange("p n j -> p (n j)"), N)
+            act = sb(f"act{t}", [P, S], F32)
+            halves = [slice(h * HALF, (h + 1) * HALF) for h in range(2)]
+            for cols in [slice(0, S)] if t < last else halves:
+                nc.scalar.activation(out=act[:, cols], in_=(drc[:, t, cols] if t < last else scaled_last[:, cols]), func=ACT.Gelu_apprx_tanh, scale=gain[t])
+            for h in range(2):
+                nc.vector.tensor_scalar(
+                    out=hid[h][:, t, :], in0=act[:, halves[h]], scalar1=unit_sb[:, t : t + 1], scalar2=None, op0=ALU.mult
+                )
 
-        hid_q = []
-        for h in range(2):
-            grouped = sb(f"hid_grouped{h}", [P, HALF, PACK], BF16)
-            copy = nc.vector.tensor_copy if h == 0 else nc.scalar.copy
+        grouped = {}
+
+        def weave(c, copy):
+            h, first = divmod(c * P, HALF)
+            grouped[c] = sb(f"hid_grouped{c}", [P, P, PACK], BF16)
             copy(
-                out=grouped[:].rearrange("p (c i) t -> p c t i", i=4),
-                in_=hid[:, :, h * HALF : (h + 1) * HALF].rearrange("p t (c i) -> p c t i", i=4),
+                out=grouped[c][:].rearrange("p (c i) t -> p c t i", i=4),
+                in_=hid[h][:, :, first : first + P].rearrange("p t (c i) -> p c t i", i=4),
             )
-            hid_q.append(quantize(f"hid{h}", grouped[:].rearrange("p n t -> p (n t)"), HALF))
 
-        for h in range(2):
-            codes, scales = hid_q[h]
-            for m in range(N // P):
-                bank = psum.tile([P, HALF], F32, name=f"out_bank{h}{m}", tag=f"y_bank{2 * h + m}")
-                product(bank[:], w3_codes, w3_scales, slice(m * P, (m + 1) * P), codes[:], scales[:])
-                result = sb(f"result{h}{m}", [P, HALF], F32)
-                copy = nc.scalar.copy if m == 0 else nc.vector.tensor_copy
-                copy(out=result[:], in_=bank[:])
-                nc.sync.dma_start(out=out[m * P : (m + 1) * P, h * HALF : (h + 1) * HALF], in_=result[:])
+        out_rows = out.rearrange("(m p) s -> p m s", p=P)
+
+        def finish(c):
+            codes, scales = quantize(f"hid{c}", grouped[c][:].rearrange("p n t -> p (n t)"), P)
+            result = sb(f"result{c}", [P, N // P, P], F32)
+            if c < 3:
+                bank = psum.tile([P, N // P, P], F32, name=f"out_bank{c}", tag=f"y_bank{c}")
+                for m in range(N // P):
+                    product(bank[:, m, :], w3_codes, w3_scales, slice(m * P, (m + 1) * P), codes[:], scales[:])
+                nc.scalar.copy(out=result[:], in_=bank[:])
+            else:
+                for m, copy in enumerate([nc.scalar.copy, nc.vector.tensor_copy]):
+                    bank = psum.tile([P, P], F32, name=f"last_bank{m}", tag=f"ye_bank{m}")
+                    product(bank[:], w3_codes, w3_scales, slice(m * P, (m + 1) * P), codes[:], scales[:])
+                    copy(out=result[:, m, :], in_=bank[:])
+            nc.sync.dma_start(out=out_rows[:, :, c * P : (c + 1) * P], in_=result[:])
+
+        weave(0, nc.vector.tensor_copy)
+        weave(1, nc.vector.tensor_copy)
+        weave(2, nc.scalar.copy)
+        weave(3, nc.scalar.copy)
+        for c in range(4):
+            finish(c)

@@ -79,6 +79,9 @@ def tile_picked_ydorax_gelu_p_kernel(
             out=drc[:, :, S], in0=ones[:], scalar1=math.sqrt(0.1 * S), scalar2=0.0, op0=ALU.mult, op1=ALU.add
         )
 
+        warm = sb("warm", [P, PACK], F32)
+        nc.scalar.activation(out=warm[:], in_=ones[:], func=ACT.Gelu_apprx_tanh)
+
         def deal_half(copy, grouped, raw, h):
             m_half = slice(h * HALF // PACK, (h + 1) * HALF // PACK)
             copy(
@@ -86,10 +89,12 @@ def tile_picked_ydorax_gelu_p_kernel(
                 in_=raw[h][:].rearrange("p j (m t) -> p m j t", t=PACK),
             )
 
-        def quantize(name, grouped_flat, width):
-            codes = sb(name + "_codes", [P, width], U32)
+        def quantize(name, grouped_flat, width, codes=None):
+            if codes is None:
+                own = sb(name + "_codes", [P, width], U32)
+                codes = own[:]
             scales = sb(name + "_scales", [P, width], U8)
-            nc.vector.quantize_mx(out=codes[:].bitcast(FP8X4), scales=scales[:], in_=grouped_flat)
+            nc.vector.quantize_mx(out=codes.bitcast(FP8X4), scales=scales[:], in_=grouped_flat)
             return codes, scales
 
         def gather(name, table, offsets, dtype):
@@ -116,7 +121,11 @@ def tile_picked_ydorax_gelu_p_kernel(
         deal_half(nc.scalar.copy, w1_grouped, w1_raw, 0)
         deal_half(nc.scalar.copy, w1_grouped, w1_raw, 1)
         e_scale_picked = gather("e_scale_picked", e_scale_table, e_list, U8)
-        w1_q = [quantize(f"w1_{t}", w1_grouped[:, t].rearrange("p m j -> p (m j)"), P) for t in range(PACK)]
+        w1_codes = sb("w1_codes", [P, H], U32, tag="e_scale_table")
+        w1_q = [
+            quantize(f"w1_{t}", w1_grouped[:, t].rearrange("p m j -> p (m j)"), P, w1_codes[:, t * P : (t + 1) * P])
+            for t in range(PACK)
+        ]
         deal_half(nc.scalar.copy, w2_grouped, w2_raw, 0)
 
         y_sb = sb("y_sb", [P, PACK, S], F32, tag="w2_raw0")
@@ -136,45 +145,30 @@ def tile_picked_ydorax_gelu_p_kernel(
         )
 
         last = PACK - 1
-        inv_nrm, gain = [], {}
-
-        def make_gain(t, tile):
-            gain[t] = tile
-            nc.vector.tensor_tensor(out=tile, in0=inv_nrm[t][:], in1=mag_sb[:, t : t + 1], op=ALU.mult)
-
+        inv_nrm = []
         for t in range(PACK):
             ye_bank = psum.tile([P, S], F32, name=f"ye_bank{t}", tag=f"ye_bank{t}")
             product(ye_bank[:], *w2_q[t], slice(0, P), e_word_picked[:], e_scale_picked[:])
             nc.vector.scalar_tensor_tensor(out=drc[:, t, :S], in0=ye_bank[:], scalar=0.7, in1=y_sb[:, t, :], op0=ALU.mult, op1=ALU.add)
-            squares = sb(f"squares{t}", [P, S + 1], F32)
+            squares = sb(f"squares{t}", [P, S + 1], F32, tag="w3_raw" if t == 0 else None)
             nrm_sq = sb(f"nrm_sq{t}", [P, 1], F32)
-            row = drc[:, t, : S + 1]
-            if t < last:
-                nc.scalar.activation(out=squares[:], in_=row, func=ACT.Square, scale=1.0 / math.sqrt(S), accum_out=nrm_sq[:])
-            else:
-                first_gain = sb("first_gain", [P, 1], F32, tag="w2_raw0")
-                make_gain(0, first_gain[:])
-                nc.vector.scalar_tensor_tensor(
-                    out=squares[:], in0=row, scalar=1.0 / S, in1=row, op0=ALU.mult, op1=ALU.mult, accum_out=nrm_sq[:]
-                )
+            nc.scalar.activation(
+                out=squares[:], in_=drc[:, t, : S + 1], func=ACT.Square, scale=1.0 / math.sqrt(S), accum_out=nrm_sq[:]
+            )
             inv_t = sb(f"inv_nrm{t}", [P, 1], F32)
             nc.gpsimd.tensor_tensor(out=inv_t[:], in0=nrm_sq[:], in1=minus_half[:], op=ALU.pow)
             inv_nrm.append(inv_t)
 
-        scaled_last = sb("scaled_last", [P, S], F32)
-        nc.vector.tensor_scalar(out=scaled_last[:], in0=drc[:, last, :S], scalar1=mag_sb[:, last:], scalar2=None, op0=ALU.mult)
-        gain[last] = inv_nrm[last][:]
-        later_gains = sb("later_gains", [P, last - 1, 8], F32, tag=f"squares{last}")
+        gain = sb("gain", [P, PACK], F32, tag="w2_raw0")
         hid = [sb(f"hid{h}", [P, PACK, HALF], BF16) for h in range(2)]
+        halves = [slice(h * HALF, (h + 1) * HALF) for h in range(2)]
         for t in range(PACK):
-            if 0 < t < last:
-                make_gain(t, later_gains[:, t - 1, 0:1])
-            if t == 1:
+            nc.vector.tensor_tensor(out=gain[:, t : t + 1], in0=inv_nrm[t][:], in1=mag_sb[:, t : t + 1], op=ALU.mult)
+            if t == 0:
                 w3_codes, w3_scales = quantize("w3", w3_grouped[:].rearrange("p n j -> p (n j)"), N)
             act = sb(f"act{t}", [P, S], F32)
-            halves = [slice(h * HALF, (h + 1) * HALF) for h in range(2)]
             for cols in [slice(0, S)] if t < last else halves:
-                nc.scalar.activation(out=act[:, cols], in_=(drc[:, t, cols] if t < last else scaled_last[:, cols]), func=ACT.Gelu_apprx_tanh, scale=gain[t])
+                nc.scalar.activation(out=act[:, cols], in_=drc[:, t, cols], func=ACT.Gelu_apprx_tanh, scale=gain[:, t : t + 1])
             for h in range(2):
                 nc.vector.tensor_scalar(
                     out=hid[h][:, t, :], in0=act[:, halves[h]], scalar1=unit_sb[:, t : t + 1], scalar2=None, op0=ALU.mult
@@ -198,12 +192,12 @@ def tile_picked_ydorax_gelu_p_kernel(
             if c < 3:
                 bank = psum.tile([P, N // P, P], F32, name=f"out_bank{c}", tag=f"y_bank{c}")
                 for m in range(N // P):
-                    product(bank[:, m, :], w3_codes, w3_scales, slice(m * P, (m + 1) * P), codes[:], scales[:])
+                    product(bank[:, m, :], w3_codes, w3_scales, slice(m * P, (m + 1) * P), codes, scales[:])
                 nc.scalar.copy(out=result[:], in_=bank[:])
             else:
                 for m, copy in enumerate([nc.scalar.copy, nc.vector.tensor_copy]):
                     bank = psum.tile([P, P], F32, name=f"last_bank{m}", tag=f"ye_bank{m}")
-                    product(bank[:], w3_codes, w3_scales, slice(m * P, (m + 1) * P), codes[:], scales[:])
+                    product(bank[:], w3_codes, w3_scales, slice(m * P, (m + 1) * P), codes, scales[:])
                     copy(out=result[:, m, :], in_=bank[:])
             nc.sync.dma_start(out=out_rows[:, :, c * P : (c + 1) * P], in_=result[:])
 

@@ -19,6 +19,7 @@ ACT = mybir.ActivationFunctionType
 P = 128
 PACK = 4
 HALF = 256
+E_PLANE = 8
 
 
 def tile_picked_ydorax_gelu_p_kernel(
@@ -38,37 +39,35 @@ def tile_picked_ydorax_gelu_p_kernel(
         e_word_table = sb("e_word_table", [P, T], U32)
         x_scale_table = sb("x_scale_table", [P, T], U8)
         e_scale_table = sb("e_scale_table", [P, T], U8)
-        w1_raw = [sb(f"w1_raw{h}", [P, PACK, HALF], F32) for h in range(2)]
-        w2_raw = [sb(f"w2_raw{h}", [P, PACK, HALF], F32) for h in range(2)]
+        w1_raw = sb("w1_raw", [P, PACK, H], F32)
+        w2_raw = sb("w2_raw", [P, PACK, H], F32)
         w3_raw = sb("w3_raw", [P, PACK, N], F32)
         mag_sb = sb("mag_sb", [P, PACK], F32)
         unit_sb = sb("unit_sb", [P, PACK], F32)
         minus_half = sb("minus_half", [P, 1], F32)
 
-        def load_scale_rows(queue, table, scales, quadrants):
+        def load_scale_rows(table, scales, first):
             rows = scales[0].bitcast(I32)
-            for q in quadrants:
-                queue.dma_start(out=table[32 * q : 32 * q + 4, :].bitcast(I32), in_=rows[4 * q : 4 * q + 4, :])
+            for r in range(4):
+                nc.sync.dma_start(out=table[first + r : P : 32, :].bitcast(I32), in_=rows[r:16:4, :])
 
         def load_words(table, words):
             nc.sync.dma_start(out=table[:].bitcast(I32), in_=words[0].rearrange("p n r -> p (n r)").bitcast(I32))
 
-        def load_half(raw, w, h):
-            nc.sync.dma_start(out=raw[h][:], in_=w.rearrange("(p j) c -> p j c", j=PACK)[:, :, h * HALF : (h + 1) * HALF])
+        def load_weights(raw, w):
+            nc.sync.dma_start(out=raw[:], in_=w.rearrange("(p j) c -> p j c", j=PACK))
 
         nc.vector.memset(x_scale_table[:].bitcast(I32), 0)
         nc.vector.memset(e_scale_table[:].bitcast(I32), 0)
         nc.sync.dma_start(x_list[:], offs)
         nc.sync.dma_start(e_list[:], adp)
         load_words(x_word_table, x_words)
-        load_scale_rows(nc.sync, x_scale_table, x_scales, range(4))
-        load_half(w1_raw, w1, 0)
-        load_half(w1_raw, w1, 1)
-        load_scale_rows(nc.sync, e_scale_table, e_scales, range(4))
-        load_half(w2_raw, w2, 0)
+        load_scale_rows(x_scale_table, x_scales, 0)
+        load_weights(w1_raw, w1)
+        load_scale_rows(e_scale_table, e_scales, E_PLANE)
         load_words(e_word_table, e_words)
-        load_half(w2_raw, w2, 1)
-        nc.sync.dma_start(out=w3_raw[:], in_=w3.rearrange("(p j) c -> p j c", j=PACK))
+        load_weights(w2_raw, w2)
+        load_weights(w3_raw, w3)
         nc.gpsimd.dma_start(out=mag_sb[:], in_=mag.rearrange("(p t) o -> p (t o)", t=PACK))
         nc.gpsimd.dma_start(out=unit_sb[:], in_=unit.rearrange("(p t) o -> p (t o)", t=PACK))
         nc.gpsimd.memset(minus_half[:], -0.5)
@@ -83,10 +82,10 @@ def tile_picked_ydorax_gelu_p_kernel(
         nc.scalar.activation(out=warm[:], in_=ones[:], func=ACT.Gelu_apprx_tanh)
 
         def deal_half(copy, grouped, raw, h):
-            m_half = slice(h * HALF // PACK, (h + 1) * HALF // PACK)
+            pair = slice(2 * h, 2 * h + 2)
             copy(
-                out=grouped[:].rearrange("p t m j -> p m j t")[:, m_half],
-                in_=raw[h][:].rearrange("p j (m t) -> p m j t", t=PACK),
+                out=grouped[h][:].rearrange("p t m j -> p m j t"),
+                in_=raw[:].rearrange("p j (m t) -> p m j t", t=PACK)[:, :, :, pair],
             )
 
         def quantize(name, grouped_flat, width, codes=None):
@@ -113,8 +112,8 @@ def tile_picked_ydorax_gelu_p_kernel(
                 stop=True,
             )
 
-        w1_grouped = sb("w1_grouped", [P, PACK, P, PACK], BF16)
-        w2_grouped = sb("w2_grouped", [P, PACK, P, PACK], BF16)
+        w1_grouped = [sb(f"w1_grouped{h}", [P, 2, P, PACK], BF16) for h in range(2)]
+        w2_grouped = [sb(f"w2_grouped{h}", [P, 2, P, PACK], BF16) for h in range(2)]
 
         x_word_picked = gather("x_word_picked", x_word_table, x_list, U32)
         x_scale_picked = gather("x_scale_picked", x_scale_table, x_list, U8)
@@ -123,20 +122,20 @@ def tile_picked_ydorax_gelu_p_kernel(
         e_scale_picked = gather("e_scale_picked", e_scale_table, e_list, U8)
         w1_codes = sb("w1_codes", [P, H], U32, tag="e_scale_table")
         w1_q = [
-            quantize(f"w1_{t}", w1_grouped[:, t].rearrange("p m j -> p (m j)"), P, w1_codes[:, t * P : (t + 1) * P])
+            quantize(f"w1_{t}", w1_grouped[t // 2][:, t % 2].rearrange("p m j -> p (m j)"), P, w1_codes[:, t * P : (t + 1) * P])
             for t in range(PACK)
         ]
-        deal_half(nc.scalar.copy, w2_grouped, w2_raw, 0)
 
-        y_sb = sb("y_sb", [P, PACK, S], F32, tag="w2_raw0")
+        y_sb = sb("y_sb", [P, PACK, S], F32)
         for t in range(PACK):
             y_bank = psum.tile([P, S], F32, name=f"y_bank{t}", tag=f"y_bank{t}")
             product(y_bank[:], *w1_q[t], slice(0, P), x_word_picked[:], x_scale_picked[:])
             nc.scalar.copy(out=y_sb[:, t, :], in_=y_bank[:])
 
         e_word_picked = gather("e_word_picked", e_word_table, e_list, U32)
+        deal_half(nc.vector.tensor_copy, w2_grouped, w2_raw, 0)
         deal_half(nc.vector.tensor_copy, w2_grouped, w2_raw, 1)
-        w2_q = [quantize(f"w2_{t}", w2_grouped[:, t].rearrange("p m j -> p (m j)"), P) for t in range(PACK)]
+        w2_q = [quantize(f"w2_{t}", w2_grouped[t // 2][:, t % 2].rearrange("p m j -> p (m j)"), P) for t in range(PACK)]
 
         w3_grouped = sb("w3_grouped", [P, N, PACK], BF16)
         nc.scalar.copy(
@@ -148,7 +147,7 @@ def tile_picked_ydorax_gelu_p_kernel(
         inv_nrm = []
         for t in range(PACK):
             ye_bank = psum.tile([P, S], F32, name=f"ye_bank{t}", tag=f"ye_bank{t}")
-            product(ye_bank[:], *w2_q[t], slice(0, P), e_word_picked[:], e_scale_picked[:])
+            product(ye_bank[:], *w2_q[t], slice(0, P), e_word_picked[:], e_scale_picked[E_PLANE:P, :])
             nc.vector.scalar_tensor_tensor(out=drc[:, t, :S], in0=ye_bank[:], scalar=0.7, in1=y_sb[:, t, :], op0=ALU.mult, op1=ALU.add)
             squares = sb(f"squares{t}", [P, S + 1], F32, tag="w3_raw" if t == 0 else None)
             nrm_sq = sb(f"nrm_sq{t}", [P, 1], F32)
@@ -159,7 +158,7 @@ def tile_picked_ydorax_gelu_p_kernel(
             nc.gpsimd.tensor_tensor(out=inv_t[:], in0=nrm_sq[:], in1=minus_half[:], op=ALU.pow)
             inv_nrm.append(inv_t)
 
-        gain = sb("gain", [P, PACK], F32, tag="w2_raw0")
+        gain = sb("gain", [P, PACK], F32, tag="y_sb")
         hid = [sb(f"hid{h}", [P, PACK, HALF], BF16) for h in range(2)]
         halves = [slice(h * HALF, (h + 1) * HALF) for h in range(2)]
         for t in range(PACK):

import math
from contextlib import ExitStack

import concourse.mybir as mybir

K, T, S, N, H = 512, 1024, 512, 256, 512
FLOPS = 2 * K * H * S * 2 + 2 * H * N * S

F32 = mybir.dt.float32
BF16 = mybir.dt.bfloat16
I32 = mybir.dt.int32
U32 = mybir.dt.uint32
U16 = mybir.dt.uint16
U8 = mybir.dt.uint8
FP8X4 = mybir.dt.float8_e4m3fn_x4
ALU = mybir.AluOpType
ACT = mybir.ActivationFunctionType

P = 128
PACK = 4
HALF = 256
E_PLANE = 8


def tile_picked_ydorax_gelu_p_kernel(
    tc, x_words, x_scales, w1, e_words, e_scales, w2, mag, unit, w3, offs, adp, out
):
    nc = tc.nc
    with ExitStack() as ctx:
        keep = ctx.enter_context(tc.tile_pool(name="keep", bufs=1))
        psum = ctx.enter_context(tc.psum_pool(name="psum", bufs=1))

        def sb(name, shape, dtype, tag=None):
            return keep.tile(shape, dtype, name=name, tag=tag or name, align_bytes=64)

        x_list = sb("x_list", [P, S // 16], U16)
        e_list = sb("e_list", [P, S // 16], U16)
        x_word_table = sb("x_word_table", [P, T], U32)
        e_word_table = sb("e_word_table", [P, T], U32)
        x_scale_table = sb("x_scale_table", [P, T], U8)
        e_scale_table = sb("e_scale_table", [P, T], U8)
        w1_raw = sb("w1_raw", [P, PACK, H], F32)
        w2_raw = sb("w2_raw", [P, PACK, H], F32)
        w3_raw = sb("w3_raw", [P, PACK, N], F32)
        mag_sb = sb("mag_sb", [P, PACK], F32)
        unit_sb = sb("unit_sb", [P, PACK], F32)
        minus_half = sb("minus_half", [P, 1], F32)

        def load_scale_rows(table, scales, first):
            rows = scales[0].bitcast(I32)
            for r in range(4):
                nc.sync.dma_start(out=table[first + r : P : 32, :].bitcast(I32), in_=rows[r:16:4, :])

        def load_words(table, words):
            nc.sync.dma_start(out=table[:].bitcast(I32), in_=words[0].rearrange("p n r -> p (n r)").bitcast(I32))

        def load_weights(raw, w):
            nc.sync.dma_start(out=raw[:], in_=w.rearrange("(p j) c -> p j c", j=PACK))

        nc.vector.memset(x_scale_table[:].bitcast(I32), 0)
        nc.vector.memset(e_scale_table[:].bitcast(I32), 0)
        nc.sync.dma_start(x_list[:], offs)
        nc.sync.dma_start(e_list[:], adp)
        load_words(x_word_table, x_words)
        load_scale_rows(x_scale_table, x_scales, 0)
        load_weights(w1_raw, w1)
        load_scale_rows(e_scale_table, e_scales, E_PLANE)
        load_words(e_word_table, e_words)
        load_weights(w2_raw, w2)
        load_weights(w3_raw, w3)
        nc.gpsimd.dma_start(out=mag_sb[:], in_=mag.rearrange("(p t) o -> p (t o)", t=PACK))
        nc.gpsimd.dma_start(out=unit_sb[:], in_=unit.rearrange("(p t) o -> p (t o)", t=PACK))
        nc.gpsimd.memset(minus_half[:], -0.5)
        drc = sb("drc", [P, PACK, S + 16], F32)
        ones = sb("ones", [P, PACK], F32)
        nc.gpsimd.memset(ones[:], 1.0)
        nc.gpsimd.tensor_scalar(
            out=drc[:, :, S], in0=ones[:], scalar1=math.sqrt(0.1 * S), scalar2=0.0, op0=ALU.mult, op1=ALU.add
        )

        warm = sb("warm", [P, PACK], F32)
        nc.scalar.activation(out=warm[:], in_=ones[:], func=ACT.Gelu_apprx_tanh)

        def deal_half(copy, grouped, raw, h):
            pair = slice(2 * h, 2 * h + 2)
            copy(
                out=grouped[h][:].rearrange("p t m j -> p m j t"),
                in_=raw[:].rearrange("p j (m t) -> p m j t", t=PACK)[:, :, :, pair],
            )

        def quantize(name, grouped_flat, width, codes=None):
            if codes is None:
                own = sb(name + "_codes", [P, width], U32)
                codes = own[:]
            scales = sb(name + "_scales", [P, width], U8)
            nc.vector.quantize_mx(out=codes.bitcast(FP8X4), scales=scales[:], in_=grouped_flat)
            return codes, scales

        def gather(name, table, offsets, dtype):
            picked = sb(name, [P, S], dtype)
            nc.vector.tensor_copy(out=picked[:], in_=table[:].indirect(offsets[:]))
            return picked

        def product(acc, w_codes, w_scales, cols, codes, scales):
            nc.tensor.matmul_mx(
                out=acc,
                lhsT=w_codes[:, cols].bitcast(FP8X4),
                lhsT_scale=w_scales[:, cols],
                rhs=codes.bitcast(FP8X4),
                rhs_scale=scales,
                start=True,
                stop=True,
            )

        w1_grouped = [sb(f"w1_grouped{h}", [P, 2, P, PACK], BF16) for h in range(2)]
        w2_grouped = [sb(f"w2_grouped{h}", [P, 2, P, PACK], BF16) for h in range(2)]

        x_word_picked = gather("x_word_picked", x_word_table, x_list, U32)
        x_scale_picked = gather("x_scale_picked", x_scale_table, x_list, U8)
        deal_half(nc.scalar.copy, w1_grouped, w1_raw, 0)
        deal_half(nc.scalar.copy, w1_grouped, w1_raw, 1)
        e_scale_picked = gather("e_scale_picked", e_scale_table, e_list, U8)
        w1_codes = sb("w1_codes", [P, H], U32, tag="e_scale_table")
        w1_q = [
            quantize(f"w1_{t}", w1_grouped[t // 2][:, t % 2].rearrange("p m j -> p (m j)"), P, w1_codes[:, t * P : (t + 1) * P])
            for t in range(PACK)
        ]

        y_sb = sb("y_sb", [P, PACK, S], F32)
        for t in range(PACK):
            y_bank = psum.tile([P, S], F32, name=f"y_bank{t}", tag=f"y_bank{t}")
            product(y_bank[:], *w1_q[t], slice(0, P), x_word_picked[:], x_scale_picked[:])
            nc.scalar.copy(out=y_sb[:, t, :], in_=y_bank[:])

        e_word_picked = gather("e_word_picked", e_word_table, e_list, U32)
        deal_half(nc.vector.tensor_copy, w2_grouped, w2_raw, 0)
        deal_half(nc.vector.tensor_copy, w2_grouped, w2_raw, 1)
        w2_q = [quantize(f"w2_{t}", w2_grouped[t // 2][:, t % 2].rearrange("p m j -> p (m j)"), P) for t in range(PACK)]

        w3_grouped = sb("w3_grouped", [P, N, PACK], BF16)
        nc.scalar.copy(
            out=w3_grouped[:].rearrange("p (c i) j -> p c j i", i=4),
            in_=w3_raw[:].rearrange("p j (c i) -> p c j i", i=4),
        )

        last = PACK - 1
        inv_nrm = []
        for t in range(PACK):
            ye_bank = psum.tile([P, S], F32, name=f"ye_bank{t}", tag=f"ye_bank{t}")
            product(ye_bank[:], *w2_q[t], slice(0, P), e_word_picked[:], e_scale_picked[E_PLANE:P, :])
            nc.vector.scalar_tensor_tensor(out=drc[:, t, :S], in0=ye_bank[:], scalar=0.7, in1=y_sb[:, t, :], op0=ALU.mult, op1=ALU.add)
            squares = sb(f"squares{t}", [P, S + 1], F32, tag="w3_raw" if t == 0 else None)
            nrm_sq = sb(f"nrm_sq{t}", [P, 1], F32)
            nc.scalar.activation(
                out=squares[:], in_=drc[:, t, : S + 1], func=ACT.Square, scale=1.0 / math.sqrt(S), accum_out=nrm_sq[:]
            )
            inv_t = sb(f"inv_nrm{t}", [P, 1], F32)
            nc.gpsimd.tensor_tensor(out=inv_t[:], in0=nrm_sq[:], in1=minus_half[:], op=ALU.pow)
            inv_nrm.append(inv_t)

        gain = sb("gain", [P, PACK], F32, tag="y_sb")
        hid = [sb(f"hid{h}", [P, PACK, HALF], BF16) for h in range(2)]
        halves = [slice(h * HALF, (h + 1) * HALF) for h in range(2)]
        for t in range(PACK):
            nc.vector.tensor_tensor(out=gain[:, t : t + 1], in0=inv_nrm[t][:], in1=mag_sb[:, t : t + 1], op=ALU.mult)
            if t == 0:
                w3_codes, w3_scales = quantize("w3", w3_grouped[:].rearrange("p n j -> p (n j)"), N)
            act = sb(f"act{t}", [P, S], F32)
            for cols in [slice(0, S)] if t < last else halves:
                nc.scalar.activation(out=act[:, cols], in_=drc[:, t, cols], func=ACT.Gelu_apprx_tanh, scale=gain[:, t : t + 1])
            for h in range(2):
                nc.vector.tensor_scalar(
                    out=hid[h][:, t, :], in0=act[:, halves[h]], scalar1=unit_sb[:, t : t + 1], scalar2=None, op0=ALU.mult
                )

        grouped = {}

        def weave(c, copy):
            h, first = divmod(c * P, HALF)
            grouped[c] = sb(f"hid_grouped{c}", [P, P, PACK], BF16)
            copy(
                out=grouped[c][:].rearrange("p (c i) t -> p c t i", i=4),
                in_=hid[h][:, :, first : first + P].rearrange("p t (c i) -> p c t i", i=4),
            )

        out_rows = out.rearrange("(m p) s -> p m s", p=P)

        def finish(c):
            codes, scales = quantize(f"hid{c}", grouped[c][:].rearrange("p n t -> p (n t)"), P)
            result = sb(f"result{c}", [P, N // P, P], F32)
            if c < 3:
                bank = psum.tile([P, N // P, P], F32, name=f"out_bank{c}", tag=f"y_bank{c}")
                for m in range(N // P):
                    product(bank[:, m, :], w3_codes, w3_scales, slice(m * P, (m + 1) * P), codes, scales[:])
                nc.scalar.copy(out=result[:], in_=bank[:])
            else:
                for m, copy in enumerate([nc.scalar.copy, nc.vector.tensor_copy]):
                    bank = psum.tile([P, P], F32, name=f"last_bank{m}", tag=f"ye_bank{m}")
                    product(bank[:], w3_codes, w3_scales, slice(m * P, (m + 1) * P), codes, scales[:])
                    copy(out=result[:, m, :], in_=bank[:])
            nc.sync.dma_start(out=out_rows[:, :, c * P : (c + 1) * P], in_=result[:])

        weave(0, nc.vector.tensor_copy)
        weave(1, nc.vector.tensor_copy)
        weave(2, nc.scalar.copy)
        weave(3, nc.scalar.copy)
        for c in range(4):
            finish(c)
